import numpy as np
import ml_dtypes


def mxq(x, axis, fmt="e4m3"):
    dtype, down = {"e4m3": (ml_dtypes.float8_e4m3fn, 7), "e5m2": (ml_dtypes.float8_e5m2, 14)}[fmt]
    v = np.moveaxis(np.asarray(x, np.float32).astype(ml_dtypes.bfloat16).astype(np.float64), axis, -1)
    blocks = v.reshape(v.shape[:-1] + (-1, 32))
    amax = np.abs(blocks).max(-1, keepdims=True)
    byte = np.maximum(np.where(amax > 0, np.frexp(amax)[1] - 1 + 127, 0) - down, 1)
    scale = np.exp2(byte - 127.0)
    codes = (blocks / scale).astype(np.float32).astype(dtype).astype(np.float64)
    return np.moveaxis((codes * scale).reshape(v.shape), -1, axis)


WIDE = False


def mx_kscale(k):
    if not WIDE:
        return np.ones(k)
    levels = np.array([30, -30])
    if k % 512:
        return np.exp2(np.random.permutation(np.resize(levels, k // 32))).repeat(32)
    a = np.empty((k // 512, 16))
    for p in range(k // 512):
        a[p, :8] = np.random.permutation(np.resize(levels, 8))
        for g in range(8):
            far = levels[np.abs(levels - a[p, g]) >= 10]
            a[p, g + 8] = far[np.random.randint(len(far))]
    return np.exp2(a.ravel()).repeat(32)


def f64(x):
    return np.asarray(x).astype(np.float64)


def striped(idx):
    return np.tile(np.asarray(idx).reshape(-1, 16).T, (8, 1)).astype(np.uint16)


def unstriped(offs):
    return offs[:16].T.reshape(-1).astype(np.int64)


def bf(x):
    return np.asarray(x, np.float32).astype(ml_dtypes.bfloat16)


def planes(Y):
    r, m = Y.shape
    b = f64(bf(Y)).reshape(r // 32, 32, m)
    amax = np.abs(b).max(1)
    byte = np.clip(np.where(amax > 0, np.frexp(amax)[1] - 1 + 127 - 7, 1), 1, 254)
    codes = (b * np.exp2(127.0 - byte)[:, None, :]).reshape(r, m).astype(np.float32).astype(ml_dtypes.float8_e4m3fn).view(np.uint8)
    words = codes.reshape(r // 512, 128, 4, m).transpose(0, 1, 3, 2)
    return np.ascontiguousarray(words), np.ascontiguousarray(byte.astype(np.uint8).reshape(r // 512, 16, m))


K, J, N, T, V, Q = 512, 512, 256, 1024, 1024, 64


def setup_inputs():
    n = np.random.standard_normal
    idx = np.random.permutation(T)[:J]
    idx2 = np.random.permutation(V)[:J]
    fj = mx_kscale(J)
    return {
        "xf": (n((K, T))).astype(np.float32),
        "ra": (np.random.uniform(0.5, 1.5, (1, J)) * fj).astype(np.float32),
        "lo": (np.random.uniform(-0.3, 0.5, (K, 1))).astype(np.float32),
        "gt": (n((N, V)) * np.exp(0.5 * n((1, V)))).astype(np.float32),
        "rb": (np.random.uniform(0.5, 1.5, (1, J)) / fj).astype(np.float32),
        "gk": (np.random.uniform(0.5, 2.0, (K, 1))).astype(np.float32),
        "offs": striped(idx),
        "offs2": striped(idx2),
    }


def reference(xf, ra, lo, gt, rb, gk, offs, offs2):
    idx = unstriped(offs)
    idx2 = unstriped(offs2)
    us = np.maximum(f64(xf)[:, idx] - f64(lo), 0.0) * f64(ra)
    uj = us.T
    gs = f64(gt)[:, idx2] * f64(rb)
    gj = gs.T
    ujq = mxq(uj, 0, "e5m2")
    gjq = mxq(gj, 0, "e5m2")
    w = ujq.T @ gjq
    wq = w.reshape(K, Q, N // Q).sum(axis=2)
    y = 0.02 * wq * f64(gk)
    words, scales = planes(y)
    return y, words, scales

@@ -1,0 +1,168 @@
+from contextlib import ExitStack
+
+import concourse.mybir as mybir
+from concourse.masks import make_identity
+
+K, J, N, T, Q = 512, 512, 256, 1024, 64
+FLOPS = 2 * K * J * N
+
+F32 = mybir.dt.float32
+BF16 = mybir.dt.bfloat16
+I32 = mybir.dt.int32
+U32 = mybir.dt.uint32
+U16 = mybir.dt.uint16
+U8 = mybir.dt.uint8
+E5M2X4 = mybir.dt.float8_e5m2_x4
+E4M3X4 = mybir.dt.float8_e4m3fn_x4
+ALU = mybir.AluOpType
+COPY = mybir.ActivationFunctionType.Copy
+AXIS_X = mybir.AxisListType.X
+
+P = 128
+PACK = 4
+GROUP = 16
+
+ORDER = [["x",0],["g",0],["x",1],["g",1],["x",2],["x",3]]
+ON_VECTOR = {"x0":256,"x3":256}
+
+
+def tile_list_moment_over_listed_sums_pl_kernel(tc, xf, ra, lo, gt, rb, gk, offs, offs2, out_0, out_1, out_2):
+    nc = tc.nc
+    with ExitStack() as ctx:
+        keep = ctx.enter_context(tc.tile_pool(name="keep", bufs=1))
+        turned = ctx.enter_context(tc.psum_pool(name="turned", bufs=1))
+        sums = ctx.enter_context(tc.psum_pool(name="sums", bufs=2))
+
+        x_list = keep.tile([P, J // GROUP], U16, name="x_list")
+        g_list = keep.tile([P, J // GROUP], U16, name="g_list")
+        lo_sb = keep.tile([P, PACK], F32, name="lo_sb")
+        ra_sb = keep.tile([P, PACK], F32, name="ra_sb")
+        rb_sb = keep.tile([P, PACK], F32, name="rb_sb")
+        gk_sb = keep.tile([P, PACK], F32, name="gk_sb")
+        ident = keep.tile([P, P], F32, name="ident")
+        make_identity(nc, ident[:])
+
+        x_rows = xf.rearrange("(c t) v -> c t v", t=PACK)
+        g_rows = gt.rearrange("(c h) v -> c h v", h=2)
+        table = {}
+        for pos, (kind, i) in enumerate(ORDER):
+            table[kind, i] = keep.tile([P, T], F32, name="table_%s%d" % (kind, i))
+            rows = x_rows if kind == "x" else g_rows
+            if pos == 0:
+                nc.sync.dma_start(x_list[:], offs)
+            if pos == 1:
+                nc.sync.dma_start(g_list[:], offs2)
+            nc.sync.dma_start(table[kind, i][:], rows[:, i, :])
+            if pos == 0:
+                nc.scalar.dma_start(lo_sb[:], lo.rearrange("(c t) o -> c (t o)", t=PACK))
+                nc.scalar.dma_start(ra_sb[:], ra.rearrange("o (p s) -> (o p) s", s=PACK))
+            if pos == 1:
+                nc.scalar.dma_start(rb_sb[:], rb.rearrange("o (p s) -> (o p) s", s=PACK))
+        nc.sync.dma_start(gk_sb[:], gk.rearrange("(c t) o -> c (t o)", t=PACK))
+
+        codes, scales, picked, bank = {}, {}, {}, {}
+
+        def gather(key):
+            kind, i = key
+            lst = x_list if kind == "x" else g_list
+            picked[key] = keep.tile([P, J], F32, name="picked_%s%d" % key)
+            cut = ON_VECTOR.get("%s%d" % key, 0)
+            if cut:
+                nc.vector.tensor_copy(picked[key][:, :cut], table[key][:].indirect(lst[:, : cut // GROUP]))
+            if cut < J:
+                nc.scalar.activation(picked[key][:, cut:], table[key][:].indirect(lst[:, cut // GROUP :]), COPY)
+
+        def turn(key):
+            kind, i = key
+            bank[key] = turned.tile([P, PACK, P], F32, name="bank_%s%d" % key)
+            if kind == "x":
+                excess = keep.tile([P, PACK, P], F32, name="excess_%d" % i)
+                nc.vector.tensor_scalar(
+                    out=excess[:].rearrange("c s (b e) -> c b s e", e=PACK),
+                    in0=picked[key][:].rearrange("c (b e s) -> c b s e", e=PACK, s=PACK),
+                    scalar1=lo_sb[:, i : i + 1],
+                    scalar2=0.0,
+                    op0=ALU.subtract,
+                    op1=ALU.max,
+                )
+                for s in range(PACK):
+                    nc.tensor.transpose(bank[key][:, s, :], excess[:, s, :], ident[:])
+            else:
+                for s in range(PACK):
+                    nc.tensor.transpose(bank[key][:, s, :], picked[key][:, s:J:PACK], ident[:])
+
+        def weigh(key):
+            kind, i = key
+            weight = ra_sb if kind == "x" else rb_sb
+            rounded = keep.tile([P, P, PACK], BF16, name="rounded_%s%d" % key, align_bytes=64)
+            nc.vector.tensor_tensor(
+                out=rounded[:],
+                in0=bank[key][:].rearrange("p s c -> p c s"),
+                in1=weight[:].unsqueeze(1).to_broadcast([P, P, PACK]),
+                op=ALU.mult,
+            )
+            codes[key] = keep.tile([P, P], U32, name="codes_%s%d" % key, align_bytes=64)
+            scales[key] = keep.tile([P, P], U8, name="scales_%s%d" % key, align_bytes=64)
+            nc.vector.quantize_mx(
+                out=codes[key][:].bitcast(E5M2X4),
+                scales=scales[key][:],
+                in_=rounded[:].rearrange("p c s -> p (c s)"),
+            )
+
+        factor = keep.tile([P, PACK], F32, name="factor")
+        nc.vector.tensor_scalar(out=factor[:], in0=gk_sb[:], scalar1=0.02, scalar2=None, op0=ALU.mult)
+        wq = keep.tile([P, PACK, Q], F32, name="wq")
+        y = keep.tile([P, PACK, Q], F32, name="y")
+
+        def moment(t):
+            acc = sums.tile([P, P], F32, name="acc")
+            for h in range(2):
+                nc.tensor.matmul_mx(
+                    out=acc[:],
+                    lhsT=codes["x", t][:].bitcast(E5M2X4),
+                    lhsT_scale=scales["x", t][:],
+                    rhs=codes["g", h][:].bitcast(E5M2X4),
+                    rhs_scale=scales["g", h][:],
+                    start=(h == 0),
+                    stop=(h == 1),
+                )
+            nc.vector.tensor_reduce(
+                out=wq[:, t, :], in_=acc[:].rearrange("p (q r) -> p q r", r=2), axis=AXIS_X, op=ALU.add
+            )
+            nc.scalar.activation(y[:, t, :], wq[:, t, :], COPY, scale=factor[:, t : t + 1])
+
+        keys = [(kind, i) for kind, i in ORDER]
+        done = set()
+        for step in range(len(keys) + 2):
+            if step < len(keys):
+                gather(keys[step])
+            if 1 <= step <= len(keys):
+                turn(keys[step - 1])
+            if step >= 2:
+                weigh(keys[step - 2])
+            if ("g", 0) in codes and ("g", 1) in codes:
+                for t in range(PACK):
+                    if ("x", t) in codes and t not in done:
+                        done.add(t)
+                        moment(t)
+
+        y_rounded = keep.tile([P, Q, PACK], BF16, name="y_rounded", align_bytes=64)
+        nc.vector.tensor_tensor(
+            out=y_rounded[:],
+            in0=wq[:].rearrange("p t q -> p q t"),
+            in1=factor[:].unsqueeze(1).to_broadcast([P, Q, PACK]),
+            op=ALU.mult,
+        )
+        y_codes = keep.tile([P, Q], U32, name="y_codes", align_bytes=64)
+        y_scales = keep.tile([P, Q], U8, name="y_scales", align_bytes=64)
+        nc.vector.quantize_mx(
+            out=y_codes[:].bitcast(E4M3X4),
+            scales=y_scales[:],
+            in_=y_rounded[:].rearrange("p q t -> p (q t)"),
+        )
+        nc.scalar.dma_start(out_0.rearrange("(p t) q -> p (t q)", t=PACK), y[:].rearrange("p t q -> p (t q)"))
+        nc.sync.dma_start(out_1.rearrange("z l c r -> (z l) (c r)").bitcast(I32), y_codes[:].bitcast(I32))
+        scale_rows = out_2.rearrange("z b c -> (z b) c").bitcast(I32)
+        for quad in range(4):
+            queue = nc.scalar if quad % 2 == 0 else nc.sync
+            queue.dma_start(scale_rows[4 * quad : 4 * quad + 4, :], y_scales[32 * quad : 32 * quad + 4, :].bitcast(I32))

@@ -22,14 +22,16 @@ P = 128
 PACK = 4
 GROUP = 16
 
-ORDER = [["x",0],["g",0],["x",1],["g",1],["x",2],["x",3]]
-ON_VECTOR = {"x0":256,"x3":256}
+ORDER = [["x",0],["g",0],["g",1],["x",1],["x",2],["x",3]]
+SORTED = [0]
+ON_VECTOR = {"x0":256,"g0":256,"g1":128,"x1":128,"x2":128,"x3":192}
 
 
 def tile_list_moment_over_listed_sums_pl_kernel(tc, xf, ra, lo, gt, rb, gk, offs, offs2, out_0, out_1, out_2):
     nc = tc.nc
     with ExitStack() as ctx:
         keep = ctx.enter_context(tc.tile_pool(name="keep", bufs=1))
+        ring = ctx.enter_context(tc.tile_pool(name="ring", bufs=2))
         turned = ctx.enter_context(tc.psum_pool(name="turned", bufs=1))
         sums = ctx.enter_context(tc.psum_pool(name="sums", bufs=2))
 
@@ -42,6 +44,11 @@ def tile_list_moment_over_listed_sums_pl_kernel(tc, xf, ra, lo, gt, rb, gk, offs
         ident = keep.tile([P, P], F32, name="ident")
         make_identity(nc, ident[:])
 
+        warm_in = keep.tile([P, 1], F32, name="warm_in")
+        warm_out = keep.tile([P, 1], F32, name="warm_out")
+        nc.vector.memset(warm_in[:], 0.0)
+        nc.scalar.activation(warm_out[:], warm_in[:], COPY)
+
         x_rows = xf.rearrange("(c t) v -> c t v", t=PACK)
         g_rows = gt.rearrange("(c h) v -> c h v", h=2)
         table = {}
@@ -49,23 +56,37 @@ def tile_list_moment_over_listed_sums_pl_kernel(tc, xf, ra, lo, gt, rb, gk, offs
             table[kind, i] = keep.tile([P, T], F32, name="table_%s%d" % (kind, i))
             rows = x_rows if kind == "x" else g_rows
             if pos == 0:
+                nc.scalar.dma_start(lo_sb[:], lo.rearrange("(c t) o -> c (t o)", t=PACK))
                 nc.sync.dma_start(x_list[:], offs)
             if pos == 1:
                 nc.sync.dma_start(g_list[:], offs2)
             nc.sync.dma_start(table[kind, i][:], rows[:, i, :])
             if pos == 0:
-                nc.scalar.dma_start(lo_sb[:], lo.rearrange("(c t) o -> c (t o)", t=PACK))
                 nc.scalar.dma_start(ra_sb[:], ra.rearrange("o (p s) -> (o p) s", s=PACK))
             if pos == 1:
                 nc.scalar.dma_start(rb_sb[:], rb.rearrange("o (p s) -> (o p) s", s=PACK))
-        nc.sync.dma_start(gk_sb[:], gk.rearrange("(c t) o -> c (t o)", t=PACK))
+        nc.gpsimd.dma_start(gk_sb[:], gk.rearrange("(c t) o -> c (t o)", t=PACK))
 
         codes, scales, picked, bank = {}, {}, {}, {}
+        minus_lo = keep.tile([P, PACK], F32, name="minus_lo")
+        nc.vector.tensor_scalar(out=minus_lo[:], in0=lo_sb[:], scalar1=-1.0, scalar2=None, op0=ALU.mult)
+        for kind, i in ORDER:
+            bank[kind, i] = turned.tile([P, PACK, P], F32, name="bank_%s%d" % (kind, i))
+            if kind == "x" and i not in SORTED:
+                for s in range(PACK):
+                    nc.tensor.matmul(
+                        bank[kind, i][:, s, :],
+                        lhsT=minus_lo[:, i : i + 1].to_broadcast([P, P]),
+                        rhs=ident[:],
+                        is_transpose=True,
+                        start=(s == 0),
+                        stop=False,
+                    )
 
         def gather(key):
             kind, i = key
             lst = x_list if kind == "x" else g_list
-            picked[key] = keep.tile([P, J], F32, name="picked_%s%d" % key)
+            picked[key] = ring.tile([P, J], F32, name="picked")
             cut = ON_VECTOR.get("%s%d" % key, 0)
             if cut:
                 nc.vector.tensor_copy(picked[key][:, :cut], table[key][:].indirect(lst[:, : cut // GROUP]))
@@ -74,8 +95,17 @@ def tile_list_moment_over_listed_sums_pl_kernel(tc, xf, ra, lo, gt, rb, gk, offs
 
         def turn(key):
             kind, i = key
-            bank[key] = turned.tile([P, PACK, P], F32, name="bank_%s%d" % key)
-            if kind == "x":
+            if kind == "x" and i not in SORTED:
+                for s in range(PACK):
+                    nc.tensor.matmul(
+                        bank[key][:, s, :],
+                        lhsT=picked[key][:, s:J:PACK],
+                        rhs=ident[:],
+                        is_transpose=True,
+                        start=False,
+                        stop=(s == PACK - 1),
+                    )
+            elif kind == "x":
                 excess = keep.tile([P, PACK, P], F32, name="excess_%d" % i)
                 nc.vector.tensor_scalar(
                     out=excess[:].rearrange("c s (b e) -> c b s e", e=PACK),
@@ -95,12 +125,22 @@ def tile_list_moment_over_listed_sums_pl_kernel(tc, xf, ra, lo, gt, rb, gk, offs
             kind, i = key
             weight = ra_sb if kind == "x" else rb_sb
             rounded = keep.tile([P, P, PACK], BF16, name="rounded_%s%d" % key, align_bytes=64)
-            nc.vector.tensor_tensor(
-                out=rounded[:],
-                in0=bank[key][:].rearrange("p s c -> p c s"),
-                in1=weight[:].unsqueeze(1).to_broadcast([P, P, PACK]),
-                op=ALU.mult,
-            )
+            if kind == "x" and i not in SORTED:
+                nc.vector.scalar_tensor_tensor(
+                    out=rounded[:],
+                    in0=bank[key][:].rearrange("p s c -> p c s"),
+                    scalar=0.0,
+                    in1=weight[:].unsqueeze(1).to_broadcast([P, P, PACK]),
+                    op0=ALU.max,
+                    op1=ALU.mult,
+                )
+            else:
+                nc.vector.tensor_tensor(
+                    out=rounded[:],
+                    in0=bank[key][:].rearrange("p s c -> p c s"),
+                    in1=weight[:].unsqueeze(1).to_broadcast([P, P, PACK]),
+                    op=ALU.mult,
+                )
             codes[key] = keep.tile([P, P], U32, name="codes_%s%d" % key, align_bytes=64)
             scales[key] = keep.tile([P, P], U8, name="scales_%s%d" % key, align_bytes=64)
             nc.vector.quantize_mx(
@@ -110,29 +150,36 @@ def tile_list_moment_over_listed_sums_pl_kernel(tc, xf, ra, lo, gt, rb, gk, offs
             )
 
         factor = keep.tile([P, PACK], F32, name="factor")
-        nc.vector.tensor_scalar(out=factor[:], in0=gk_sb[:], scalar1=0.02, scalar2=None, op0=ALU.mult)
+        nc.gpsimd.tensor_scalar(out=factor[:], in0=gk_sb[:], scalar1=0.02, scalar2=0.0, op0=ALU.mult, op1=ALU.add)
         wq = keep.tile([P, PACK, Q], F32, name="wq")
         y = keep.tile([P, PACK, Q], F32, name="y")
 
-        def moment(t):
-            acc = sums.tile([P, P], F32, name="acc")
-            for h in range(2):
-                nc.tensor.matmul_mx(
-                    out=acc[:],
-                    lhsT=codes["x", t][:].bitcast(E5M2X4),
-                    lhsT_scale=scales["x", t][:],
-                    rhs=codes["g", h][:].bitcast(E5M2X4),
-                    rhs_scale=scales["g", h][:],
-                    start=(h == 0),
-                    stop=(h == 1),
-                )
+        y_rounded = keep.tile([P, Q, PACK], BF16, name="y_rounded", align_bytes=64)
+
+        def moment(slices, pool, tag):
+            acc = pool.tile([P, len(slices), P], F32, name=tag)
+            for n, t in enumerate(slices):
+                for h in range(2):
+                    nc.tensor.matmul_mx(
+                        out=acc[:, n, :],
+                        lhsT=codes["x", t][:].bitcast(E5M2X4),
+                        lhsT_scale=scales["x", t][:],
+                        rhs=codes["g", h][:].bitcast(E5M2X4),
+                        rhs_scale=scales["g", h][:],
+                        start=(h == 0),
+                        stop=(h == 1),
+                    )
             nc.vector.tensor_reduce(
-                out=wq[:, t, :], in_=acc[:].rearrange("p (q r) -> p q r", r=2), axis=AXIS_X, op=ALU.add
+                out=wq[:, slices[0] : slices[-1] + 1, :],
+                in_=acc[:].rearrange("p n (q r) -> p n q r", r=2),
+                axis=AXIS_X,
+                op=ALU.add,
             )
-            nc.scalar.activation(y[:, t, :], wq[:, t, :], COPY, scale=factor[:, t : t + 1])
+            for t in slices:
+                nc.scalar.activation(y_rounded[:, :, t], wq[:, t, :], COPY, scale=factor[:, t : t + 1])
+                nc.scalar.activation(y[:, t, :], wq[:, t, :], COPY, scale=factor[:, t : t + 1])
 
         keys = [(kind, i) for kind, i in ORDER]
-        done = set()
         for step in range(len(keys) + 2):
             if step < len(keys):
                 gather(keys[step])
@@ -140,19 +187,10 @@ def tile_list_moment_over_listed_sums_pl_kernel(tc, xf, ra, lo, gt, rb, gk, offs
                 turn(keys[step - 1])
             if step >= 2:
                 weigh(keys[step - 2])
-            if ("g", 0) in codes and ("g", 1) in codes:
-                for t in range(PACK):
-                    if ("x", t) in codes and t not in done:
-                        done.add(t)
-                        moment(t)
+        moment([0, 1], turned, "bank_x2")
+        moment([2], sums, "acc")
+        moment([3], sums, "acc")
 
-        y_rounded = keep.tile([P, Q, PACK], BF16, name="y_rounded", align_bytes=64)
-        nc.vector.tensor_tensor(
-            out=y_rounded[:],
-            in0=wq[:].rearrange("p t q -> p q t"),
-            in1=factor[:].unsqueeze(1).to_broadcast([P, Q, PACK]),
-            op=ALU.mult,
-        )
         y_codes = keep.tile([P, Q], U32, name="y_codes", align_bytes=64)
         y_scales = keep.tile([P, Q], U8, name="y_scales", align_bytes=64)
         nc.vector.quantize_mx(

@@ -57,15 +57,15 @@ def tile_list_moment_over_listed_sums_pl_kernel(tc, xf, ra, lo, gt, rb, gk, offs
             rows = x_rows if kind == "x" else g_rows
             if pos == 0:
                 nc.scalar.dma_start(lo_sb[:], lo.rearrange("(c t) o -> c (t o)", t=PACK))
-                nc.sync.dma_start(x_list[:], offs)
-            if pos == 1:
-                nc.sync.dma_start(g_list[:], offs2)
             nc.sync.dma_start(table[kind, i][:], rows[:, i, :])
+            if pos == 0:
+                nc.sync.dma_start(x_list[:], offs)
+                nc.sync.dma_start(g_list[:], offs2)
             if pos == 0:
                 nc.scalar.dma_start(ra_sb[:], ra.rearrange("o (p s) -> (o p) s", s=PACK))
             if pos == 1:
                 nc.scalar.dma_start(rb_sb[:], rb.rearrange("o (p s) -> (o p) s", s=PACK))
-        nc.gpsimd.dma_start(gk_sb[:], gk.rearrange("(c t) o -> c (t o)", t=PACK))
+        nc.sync.dma_start(gk_sb[:], gk.rearrange("(c t) o -> c (t o)", t=PACK))
 
         codes, scales, picked, bank = {}, {}, {}, {}
         minus_lo = keep.tile([P, PACK], F32, name="minus_lo")
@@ -176,7 +176,8 @@ def tile_list_moment_over_listed_sums_pl_kernel(tc, xf, ra, lo, gt, rb, gk, offs
                 op=ALU.add,
             )
             for t in slices:
-                nc.scalar.activation(y_rounded[:, :, t], wq[:, t, :], COPY, scale=factor[:, t : t + 1])
+                if t >= 2:
+                    nc.scalar.activation(y_rounded[:, :, t], wq[:, t, :], COPY, scale=factor[:, t : t + 1])
                 nc.scalar.activation(y[:, t, :], wq[:, t, :], COPY, scale=factor[:, t : t + 1])
 
         keys = [(kind, i) for kind, i in ORDER]
@@ -189,6 +190,14 @@ def tile_list_moment_over_listed_sums_pl_kernel(tc, xf, ra, lo, gt, rb, gk, offs
                 weigh(keys[step - 2])
         moment([0, 1], turned, "bank_x2")
         moment([2], sums, "acc")
+        nc.vector.tensor_tensor(
+            out=y_rounded[:, :, 0:2],
+            in0=wq[:, 0:2, :].rearrange("p t q -> p q t"),
+            in1=factor[:, 0:2].unsqueeze(1).to_broadcast([P, Q, 2]),
+            op=ALU.mult,
+        )
+        y_rows = out_0.rearrange("(p t) q -> p t q", t=PACK)
+        nc.sync.dma_start(y_rows[:, 0:3, :], y[:, 0:3, :])
         moment([3], sums, "acc")
 
         y_codes = keep.tile([P, Q], U32, name="y_codes", align_bytes=64)
@@ -198,9 +207,9 @@ def tile_list_moment_over_listed_sums_pl_kernel(tc, xf, ra, lo, gt, rb, gk, offs
             scales=y_scales[:],
             in_=y_rounded[:].rearrange("p q t -> p (q t)"),
         )
-        nc.scalar.dma_start(out_0.rearrange("(p t) q -> p (t q)", t=PACK), y[:].rearrange("p t q -> p (t q)"))
+        nc.sync.dma_start(y_rows[:, 3, :], y[:, 3, :])
         nc.sync.dma_start(out_1.rearrange("z l c r -> (z l) (c r)").bitcast(I32), y_codes[:].bitcast(I32))
         scale_rows = out_2.rearrange("z b c -> (z b) c").bitcast(I32)
         for quad in range(4):
-            queue = nc.scalar if quad % 2 == 0 else nc.sync
+            queue = nc.scalar if quad < 3 else nc.sync
             queue.dma_start(scale_rows[4 * quad : 4 * quad + 4, :], y_scales[32 * quad : 32 * quad + 4, :].bitcast(I32))

@@ -20,11 +20,21 @@ AXIS_X = mybir.AxisListType.X
 
 P = 128
 PACK = 4
+G_TILES = 2
 GROUP = 16
+QUADRANT = 32
+SCALE_ROWS = 4
 
-ORDER = [["x",0],["g",0],["g",1],["x",1],["x",2],["x",3]]
-SORTED = [0]
-ON_VECTOR = {"x0":256,"g0":256,"g1":128,"x1":128,"x2":128,"x3":192}
+FIRST_X = ("x", 0)
+TILES = [FIRST_X] + [("g", h) for h in range(G_TILES)] + [("x", t) for t in range(1, PACK)]
+
+VECTOR_ENTRIES_HEAD, VECTOR_ENTRIES_MIDDLE, VECTOR_ENTRIES_LAST = 256, 128, 192
+
+
+def vector_entries(position):
+    if position < 2:
+        return VECTOR_ENTRIES_HEAD
+    return VECTOR_ENTRIES_LAST if position == len(TILES) - 1 else VECTOR_ENTRIES_MIDDLE
 
 
 def tile_list_moment_over_listed_sums_pl_kernel(tc, xf, ra, lo, gt, rb, gk, offs, offs2, out_0, out_1, out_2):
@@ -49,33 +59,36 @@ def tile_list_moment_over_listed_sums_pl_kernel(tc, xf, ra, lo, gt, rb, gk, offs
         nc.vector.memset(warm_in[:], 0.0)
         nc.scalar.activation(warm_out[:], warm_in[:], COPY)
 
-        x_rows = xf.rearrange("(c t) v -> c t v", t=PACK)
-        g_rows = gt.rearrange("(c h) v -> c h v", h=2)
-        table = {}
-        for pos, (kind, i) in enumerate(ORDER):
-            table[kind, i] = keep.tile([P, T], F32, name="table_%s%d" % (kind, i))
-            rows = x_rows if kind == "x" else g_rows
-            if pos == 0:
-                nc.scalar.dma_start(lo_sb[:], lo.rearrange("(c t) o -> c (t o)", t=PACK))
-            nc.sync.dma_start(table[kind, i][:], rows[:, i, :])
-            if pos == 0:
-                nc.sync.dma_start(x_list[:], offs)
-                nc.sync.dma_start(g_list[:], offs2)
-            if pos == 0:
-                nc.scalar.dma_start(ra_sb[:], ra.rearrange("o (p s) -> (o p) s", s=PACK))
-            if pos == 1:
-                nc.scalar.dma_start(rb_sb[:], rb.rearrange("o (p s) -> (o p) s", s=PACK))
+        rows = {
+            "x": xf.rearrange("(c t) v -> c t v", t=PACK),
+            "g": gt.rearrange("(c h) v -> c h v", h=G_TILES),
+        }
+        table = {key: keep.tile([P, T], F32, name="table_%s%d" % key) for key in TILES}
+
+        def load_table(key):
+            nc.sync.dma_start(table[key][:], rows[key[0]][:, key[1], :])
+
+        nc.scalar.dma_start(lo_sb[:], lo.rearrange("(c t) o -> c (t o)", t=PACK))
+        load_table(TILES[0])
+        nc.sync.dma_start(x_list[:], offs)
+        nc.sync.dma_start(g_list[:], offs2)
+        nc.scalar.dma_start(ra_sb[:], ra.rearrange("o (p s) -> (o p) s", s=PACK))
+        load_table(TILES[1])
+        nc.scalar.dma_start(rb_sb[:], rb.rearrange("o (p s) -> (o p) s", s=PACK))
+        for key in TILES[2:]:
+            load_table(key)
         nc.sync.dma_start(gk_sb[:], gk.rearrange("(c t) o -> c (t o)", t=PACK))
 
-        codes, scales, picked, bank = {}, {}, {}, {}
         minus_lo = keep.tile([P, PACK], F32, name="minus_lo")
         nc.vector.tensor_scalar(out=minus_lo[:], in0=lo_sb[:], scalar1=-1.0, scalar2=None, op0=ALU.mult)
-        for kind, i in ORDER:
-            bank[kind, i] = turned.tile([P, PACK, P], F32, name="bank_%s%d" % (kind, i))
-            if kind == "x" and i not in SORTED:
+        bank = {}
+        for key in TILES:
+            kind, i = key
+            bank[key] = turned.tile([P, PACK, P], F32, name="bank_%s%d" % key)
+            if kind == "x" and key != FIRST_X:
                 for s in range(PACK):
                     nc.tensor.matmul(
-                        bank[kind, i][:, s, :],
+                        bank[key][:, s, :],
                         lhsT=minus_lo[:, i : i + 1].to_broadcast([P, P]),
                         rhs=ident[:],
                         is_transpose=True,
@@ -83,30 +96,33 @@ def tile_list_moment_over_listed_sums_pl_kernel(tc, xf, ra, lo, gt, rb, gk, offs
                         stop=False,
                     )
 
-        def gather(key):
-            kind, i = key
-            lst = x_list if kind == "x" else g_list
+        rounded, codes, scales, call_after = {}, {}, {}, {}
+        for batch in [TILES[:1], TILES[1 : 1 + G_TILES]] + [[key] for key in TILES[1 + G_TILES :]]:
+            width = P * len(batch)
+            batch_rounded = keep.tile([P, width, PACK], BF16, name="rounded_%s%d" % batch[0], align_bytes=64)
+            batch_codes = keep.tile([P, width], U32, name="codes_%s%d" % batch[0], align_bytes=64)
+            batch_scales = keep.tile([P, width], U8, name="scales_%s%d" % batch[0], align_bytes=64)
+            for place, key in enumerate(batch):
+                columns = slice(place * P, (place + 1) * P)
+                rounded[key] = batch_rounded[:, columns, :]
+                codes[key] = batch_codes[:, columns]
+                scales[key] = batch_scales[:, columns]
+            call_after[batch[-1]] = (batch_rounded, batch_codes, batch_scales)
+
+        picked = {}
+
+        def gather(position):
+            key = TILES[position]
+            entries = x_list if key[0] == "x" else g_list
             picked[key] = ring.tile([P, J], F32, name="picked")
-            cut = ON_VECTOR.get("%s%d" % key, 0)
-            if cut:
-                nc.vector.tensor_copy(picked[key][:, :cut], table[key][:].indirect(lst[:, : cut // GROUP]))
-            if cut < J:
-                nc.scalar.activation(picked[key][:, cut:], table[key][:].indirect(lst[:, cut // GROUP :]), COPY)
+            cut = vector_entries(position)
+            nc.vector.tensor_copy(picked[key][:, :cut], table[key][:].indirect(entries[:, : cut // GROUP]))
+            nc.scalar.activation(picked[key][:, cut:], table[key][:].indirect(entries[:, cut // GROUP :]), COPY)
 
         def turn(key):
             kind, i = key
-            if kind == "x" and i not in SORTED:
-                for s in range(PACK):
-                    nc.tensor.matmul(
-                        bank[key][:, s, :],
-                        lhsT=picked[key][:, s:J:PACK],
-                        rhs=ident[:],
-                        is_transpose=True,
-                        start=False,
-                        stop=(s == PACK - 1),
-                    )
-            elif kind == "x":
-                excess = keep.tile([P, PACK, P], F32, name="excess_%d" % i)
+            if key == FIRST_X:
+                excess = keep.tile([P, PACK, P], F32, name="excess")
                 nc.vector.tensor_scalar(
                     out=excess[:].rearrange("c s (b e) -> c b s e", e=PACK),
                     in0=picked[key][:].rearrange("c (b e s) -> c b s e", e=PACK, s=PACK),
@@ -117,79 +133,76 @@ def tile_list_moment_over_listed_sums_pl_kernel(tc, xf, ra, lo, gt, rb, gk, offs
                 )
                 for s in range(PACK):
                     nc.tensor.transpose(bank[key][:, s, :], excess[:, s, :], ident[:])
+            elif kind == "x":
+                for s in range(PACK):
+                    nc.tensor.matmul(
+                        bank[key][:, s, :],
+                        lhsT=picked[key][:, s:J:PACK],
+                        rhs=ident[:],
+                        is_transpose=True,
+                        start=False,
+                        stop=(s == PACK - 1),
+                    )
             else:
                 for s in range(PACK):
                     nc.tensor.transpose(bank[key][:, s, :], picked[key][:, s:J:PACK], ident[:])
 
         def weigh(key):
-            kind, i = key
-            weight = ra_sb if kind == "x" else rb_sb
-            rounded = keep.tile([P, P, PACK], BF16, name="rounded_%s%d" % key, align_bytes=64)
-            if kind == "x" and i not in SORTED:
+            weight = (ra_sb if key[0] == "x" else rb_sb)[:].unsqueeze(1).to_broadcast([P, P, PACK])
+            values = bank[key][:].rearrange("p s c -> p c s")
+            if key[0] == "x" and key != FIRST_X:
                 nc.vector.scalar_tensor_tensor(
-                    out=rounded[:],
-                    in0=bank[key][:].rearrange("p s c -> p c s"),
-                    scalar=0.0,
-                    in1=weight[:].unsqueeze(1).to_broadcast([P, P, PACK]),
-                    op0=ALU.max,
-                    op1=ALU.mult,
+                    out=rounded[key], in0=values, scalar=0.0, in1=weight, op0=ALU.max, op1=ALU.mult
                 )
             else:
-                nc.vector.tensor_tensor(
-                    out=rounded[:],
-                    in0=bank[key][:].rearrange("p s c -> p c s"),
-                    in1=weight[:].unsqueeze(1).to_broadcast([P, P, PACK]),
-                    op=ALU.mult,
+                nc.vector.tensor_tensor(out=rounded[key], in0=values, in1=weight, op=ALU.mult)
+            if key in call_after:
+                batch_rounded, batch_codes, batch_scales = call_after[key]
+                nc.vector.quantize_mx(
+                    out=batch_codes[:].bitcast(E5M2X4),
+                    scales=batch_scales[:],
+                    in_=batch_rounded[:].rearrange("p c s -> p (c s)"),
                 )
-            codes[key] = keep.tile([P, P], U32, name="codes_%s%d" % key, align_bytes=64)
-            scales[key] = keep.tile([P, P], U8, name="scales_%s%d" % key, align_bytes=64)
-            nc.vector.quantize_mx(
-                out=codes[key][:].bitcast(E5M2X4),
-                scales=scales[key][:],
-                in_=rounded[:].rearrange("p c s -> p (c s)"),
-            )
 
         factor = keep.tile([P, PACK], F32, name="factor")
         nc.gpsimd.tensor_scalar(out=factor[:], in0=gk_sb[:], scalar1=0.02, scalar2=0.0, op0=ALU.mult, op1=ALU.add)
         wq = keep.tile([P, PACK, Q], F32, name="wq")
         y = keep.tile([P, PACK, Q], F32, name="y")
-
         y_rounded = keep.tile([P, Q, PACK], BF16, name="y_rounded", align_bytes=64)
 
-        def moment(slices, pool, tag):
-            acc = pool.tile([P, len(slices), P], F32, name=tag)
-            for n, t in enumerate(slices):
-                for h in range(2):
+        def moment(x_tiles, acc):
+            for place, t in enumerate(x_tiles):
+                for h in range(G_TILES):
                     nc.tensor.matmul_mx(
-                        out=acc[:, n, :],
-                        lhsT=codes["x", t][:].bitcast(E5M2X4),
-                        lhsT_scale=scales["x", t][:],
-                        rhs=codes["g", h][:].bitcast(E5M2X4),
-                        rhs_scale=scales["g", h][:],
+                        out=acc[:, place, :],
+                        lhsT=codes["x", t].bitcast(E5M2X4),
+                        lhsT_scale=scales["x", t],
+                        rhs=codes["g", h].bitcast(E5M2X4),
+                        rhs_scale=scales["g", h],
                         start=(h == 0),
-                        stop=(h == 1),
+                        stop=(h == G_TILES - 1),
                     )
             nc.vector.tensor_reduce(
-                out=wq[:, slices[0] : slices[-1] + 1, :],
-                in_=acc[:].rearrange("p n (q r) -> p n q r", r=2),
+                out=wq[:, x_tiles[0] : x_tiles[-1] + 1, :],
+                in_=acc[:].rearrange("p m (q r) -> p m q r", r=2),
                 axis=AXIS_X,
                 op=ALU.add,
             )
-            for t in slices:
+            for t in x_tiles:
                 if t >= 2:
                     nc.scalar.activation(y_rounded[:, :, t], wq[:, t, :], COPY, scale=factor[:, t : t + 1])
                 nc.scalar.activation(y[:, t, :], wq[:, t, :], COPY, scale=factor[:, t : t + 1])
 
-        keys = [(kind, i) for kind, i in ORDER]
-        for step in range(len(keys) + 2):
-            if step < len(keys):
-                gather(keys[step])
-            if 1 <= step <= len(keys):
-                turn(keys[step - 1])
+        for step in range(len(TILES) + 2):
+            if step < len(TILES):
+                gather(step)
+            if 1 <= step <= len(TILES):
+                turn(TILES[step - 1])
             if step >= 2:
-                weigh(keys[step - 2])
-        moment([0, 1], turned, "bank_x2")
-        moment([2], sums, "acc")
+                weigh(TILES[step - 2])
+
+        moment([0, 1], turned.tile([P, 2, P], F32, name="bank_x1"))
+        moment([2], sums.tile([P, 1, P], F32, name="acc"))
         nc.vector.tensor_tensor(
             out=y_rounded[:, :, 0:2],
             in0=wq[:, 0:2, :].rearrange("p t q -> p q t"),
@@ -198,7 +211,7 @@ def tile_list_moment_over_listed_sums_pl_kernel(tc, xf, ra, lo, gt, rb, gk, offs
         )
         y_rows = out_0.rearrange("(p t) q -> p t q", t=PACK)
         nc.sync.dma_start(y_rows[:, 0:3, :], y[:, 0:3, :])
-        moment([3], sums, "acc")
+        moment([3], sums.tile([P, 1, P], F32, name="acc"))
 
         y_codes = keep.tile([P, Q], U32, name="y_codes", align_bytes=64)
         y_scales = keep.tile([P, Q], U8, name="y_scales", align_bytes=64)
@@ -207,9 +220,13 @@ def tile_list_moment_over_listed_sums_pl_kernel(tc, xf, ra, lo, gt, rb, gk, offs
             scales=y_scales[:],
             in_=y_rounded[:].rearrange("p q t -> p (q t)"),
         )
+
         nc.sync.dma_start(y_rows[:, 3, :], y[:, 3, :])
         nc.sync.dma_start(out_1.rearrange("z l c r -> (z l) (c r)").bitcast(I32), y_codes[:].bitcast(I32))
         scale_rows = out_2.rearrange("z b c -> (z b) c").bitcast(I32)
-        for quad in range(4):
+        for quad in range(P // QUADRANT):
             queue = nc.scalar if quad < 3 else nc.sync
-            queue.dma_start(scale_rows[4 * quad : 4 * quad + 4, :], y_scales[32 * quad : 32 * quad + 4, :].bitcast(I32))
+            queue.dma_start(
+                scale_rows[SCALE_ROWS * quad : SCALE_ROWS * (quad + 1), :],
+                y_scales[QUADRANT * quad : QUADRANT * quad + SCALE_ROWS, :].bitcast(I32),
+            )

from contextlib import ExitStack

import concourse.mybir as mybir
from concourse.masks import make_identity

K, J, N, T, Q = 512, 512, 256, 1024, 64
FLOPS = 2 * K * J * N

F32 = mybir.dt.float32
BF16 = mybir.dt.bfloat16
I32 = mybir.dt.int32
U32 = mybir.dt.uint32
U16 = mybir.dt.uint16
U8 = mybir.dt.uint8
E5M2X4 = mybir.dt.float8_e5m2_x4
E4M3X4 = mybir.dt.float8_e4m3fn_x4
ALU = mybir.AluOpType
COPY = mybir.ActivationFunctionType.Copy
AXIS_X = mybir.AxisListType.X

P = 128
PACK = 4
G_TILES = 2
GROUP = 16
QUADRANT = 32
SCALE_ROWS = 4

FIRST_X = ("x", 0)
TILES = [FIRST_X] + [("g", h) for h in range(G_TILES)] + [("x", t) for t in range(1, PACK)]

VECTOR_ENTRIES_HEAD, VECTOR_ENTRIES_MIDDLE, VECTOR_ENTRIES_LAST = 256, 128, 192


def vector_entries(position):
    if position < 2:
        return VECTOR_ENTRIES_HEAD
    return VECTOR_ENTRIES_LAST if position == len(TILES) - 1 else VECTOR_ENTRIES_MIDDLE


def tile_list_moment_over_listed_sums_pl_kernel(tc, xf, ra, lo, gt, rb, gk, offs, offs2, out_0, out_1, out_2):
    nc = tc.nc
    with ExitStack() as ctx:
        keep = ctx.enter_context(tc.tile_pool(name="keep", bufs=1))
        ring = ctx.enter_context(tc.tile_pool(name="ring", bufs=2))
        turned = ctx.enter_context(tc.psum_pool(name="turned", bufs=1))
        sums = ctx.enter_context(tc.psum_pool(name="sums", bufs=2))

        x_list = keep.tile([P, J // GROUP], U16, name="x_list")
        g_list = keep.tile([P, J // GROUP], U16, name="g_list")
        lo_sb = keep.tile([P, PACK], F32, name="lo_sb")
        ra_sb = keep.tile([P, PACK], F32, name="ra_sb")
        rb_sb = keep.tile([P, PACK], F32, name="rb_sb")
        gk_sb = keep.tile([P, PACK], F32, name="gk_sb")
        ident = keep.tile([P, P], F32, name="ident")
        make_identity(nc, ident[:])

        warm_in = keep.tile([P, 1], F32, name="warm_in")
        warm_out = keep.tile([P, 1], F32, name="warm_out")
        nc.vector.memset(warm_in[:], 0.0)
        nc.scalar.activation(warm_out[:], warm_in[:], COPY)

        rows = {
            "x": xf.rearrange("(c t) v -> c t v", t=PACK),
            "g": gt.rearrange("(c h) v -> c h v", h=G_TILES),
        }
        table = {key: keep.tile([P, T], F32, name="table_%s%d" % key) for key in TILES}

        def load_table(key):
            nc.sync.dma_start(table[key][:], rows[key[0]][:, key[1], :])

        nc.scalar.dma_start(lo_sb[:], lo.rearrange("(c t) o -> c (t o)", t=PACK))
        load_table(TILES[0])
        nc.sync.dma_start(x_list[:], offs)
        nc.sync.dma_start(g_list[:], offs2)
        nc.scalar.dma_start(ra_sb[:], ra.rearrange("o (p s) -> (o p) s", s=PACK))
        load_table(TILES[1])
        nc.scalar.dma_start(rb_sb[:], rb.rearrange("o (p s) -> (o p) s", s=PACK))
        for key in TILES[2:]:
            load_table(key)
        nc.sync.dma_start(gk_sb[:], gk.rearrange("(c t) o -> c (t o)", t=PACK))

        minus_lo = keep.tile([P, PACK], F32, name="minus_lo")
        nc.vector.tensor_scalar(out=minus_lo[:], in0=lo_sb[:], scalar1=-1.0, scalar2=None, op0=ALU.mult)
        bank = {}
        for key in TILES:
            kind, i = key
            bank[key] = turned.tile([P, PACK, P], F32, name="bank_%s%d" % key)
            if kind == "x" and key != FIRST_X:
                for s in range(PACK):
                    nc.tensor.matmul(
                        bank[key][:, s, :],
                        lhsT=minus_lo[:, i : i + 1].to_broadcast([P, P]),
                        rhs=ident[:],
                        is_transpose=True,
                        start=(s == 0),
                        stop=False,
                    )

        rounded, codes, scales, call_after = {}, {}, {}, {}
        for batch in [TILES[:1], TILES[1 : 1 + G_TILES]] + [[key] for key in TILES[1 + G_TILES :]]:
            width = P * len(batch)
            batch_rounded = keep.tile([P, width, PACK], BF16, name="rounded_%s%d" % batch[0], align_bytes=64)
            batch_codes = keep.tile([P, width], U32, name="codes_%s%d" % batch[0], align_bytes=64)
            batch_scales = keep.tile([P, width], U8, name="scales_%s%d" % batch[0], align_bytes=64)
            for place, key in enumerate(batch):
                columns = slice(place * P, (place + 1) * P)
                rounded[key] = batch_rounded[:, columns, :]
                codes[key] = batch_codes[:, columns]
                scales[key] = batch_scales[:, columns]
            call_after[batch[-1]] = (batch_rounded, batch_codes, batch_scales)

        picked = {}

        def gather(position):
            key = TILES[position]
            entries = x_list if key[0] == "x" else g_list
            picked[key] = ring.tile([P, J], F32, name="picked")
            cut = vector_entries(position)
            nc.vector.tensor_copy(picked[key][:, :cut], table[key][:].indirect(entries[:, : cut // GROUP]))
            nc.scalar.activation(picked[key][:, cut:], table[key][:].indirect(entries[:, cut // GROUP :]), COPY)

        def turn(key):
            kind, i = key
            if key == FIRST_X:
                excess = keep.tile([P, PACK, P], F32, name="excess")
                nc.vector.tensor_scalar(
                    out=excess[:].rearrange("c s (b e) -> c b s e", e=PACK),
                    in0=picked[key][:].rearrange("c (b e s) -> c b s e", e=PACK, s=PACK),
                    scalar1=lo_sb[:, i : i + 1],
                    scalar2=0.0,
                    op0=ALU.subtract,
                    op1=ALU.max,
                )
                for s in range(PACK):
                    nc.tensor.transpose(bank[key][:, s, :], excess[:, s, :], ident[:])
            elif kind == "x":
                for s in range(PACK):
                    nc.tensor.matmul(
                        bank[key][:, s, :],
                        lhsT=picked[key][:, s:J:PACK],
                        rhs=ident[:],
                        is_transpose=True,
                        start=False,
                        stop=(s == PACK - 1),
                    )
            else:
                for s in range(PACK):
                    nc.tensor.transpose(bank[key][:, s, :], picked[key][:, s:J:PACK], ident[:])

        def weigh(key):
            weight = (ra_sb if key[0] == "x" else rb_sb)[:].unsqueeze(1).to_broadcast([P, P, PACK])
            values = bank[key][:].rearrange("p s c -> p c s")
            if key[0] == "x" and key != FIRST_X:
                nc.vector.scalar_tensor_tensor(
                    out=rounded[key], in0=values, scalar=0.0, in1=weight, op0=ALU.max, op1=ALU.mult
                )
            else:
                nc.vector.tensor_tensor(out=rounded[key], in0=values, in1=weight, op=ALU.mult)
            if key in call_after:
                batch_rounded, batch_codes, batch_scales = call_after[key]
                nc.vector.quantize_mx(
                    out=batch_codes[:].bitcast(E5M2X4),
                    scales=batch_scales[:],
                    in_=batch_rounded[:].rearrange("p c s -> p (c s)"),
                )

        factor = keep.tile([P, PACK], F32, name="factor")
        nc.gpsimd.tensor_scalar(out=factor[:], in0=gk_sb[:], scalar1=0.02, scalar2=0.0, op0=ALU.mult, op1=ALU.add)
        wq = keep.tile([P, PACK, Q], F32, name="wq")
        y = keep.tile([P, PACK, Q], F32, name="y")
        y_rounded = keep.tile([P, Q, PACK], BF16, name="y_rounded", align_bytes=64)

        def moment(x_tiles, acc):
            for place, t in enumerate(x_tiles):
                for h in range(G_TILES):
                    nc.tensor.matmul_mx(
                        out=acc[:, place, :],
                        lhsT=codes["x", t].bitcast(E5M2X4),
                        lhsT_scale=scales["x", t],
                        rhs=codes["g", h].bitcast(E5M2X4),
                        rhs_scale=scales["g", h],
                        start=(h == 0),
                        stop=(h == G_TILES - 1),
                    )
            nc.vector.tensor_reduce(
                out=wq[:, x_tiles[0] : x_tiles[-1] + 1, :],
                in_=acc[:].rearrange("p m (q r) -> p m q r", r=2),
                axis=AXIS_X,
                op=ALU.add,
            )
            for t in x_tiles:
                if t >= 2:
                    nc.scalar.activation(y_rounded[:, :, t], wq[:, t, :], COPY, scale=factor[:, t : t + 1])
                nc.scalar.activation(y[:, t, :], wq[:, t, :], COPY, scale=factor[:, t : t + 1])

        for step in range(len(TILES) + 2):
            if step < len(TILES):
                gather(step)
            if 1 <= step <= len(TILES):
                turn(TILES[step - 1])
            if step >= 2:
                weigh(TILES[step - 2])

        moment([0, 1], turned.tile([P, 2, P], F32, name="bank_x1"))
        moment([2], sums.tile([P, 1, P], F32, name="acc"))
        nc.vector.tensor_tensor(
            out=y_rounded[:, :, 0:2],
            in0=wq[:, 0:2, :].rearrange("p t q -> p q t"),
            in1=factor[:, 0:2].unsqueeze(1).to_broadcast([P, Q, 2]),
            op=ALU.mult,
        )
        y_rows = out_0.rearrange("(p t) q -> p t q", t=PACK)
        nc.sync.dma_start(y_rows[:, 0:3, :], y[:, 0:3, :])
        moment([3], sums.tile([P, 1, P], F32, name="acc"))

        y_codes = keep.tile([P, Q], U32, name="y_codes", align_bytes=64)
        y_scales = keep.tile([P, Q], U8, name="y_scales", align_bytes=64)
        nc.vector.quantize_mx(
            out=y_codes[:].bitcast(E4M3X4),
            scales=y_scales[:],
            in_=y_rounded[:].rearrange("p q t -> p (q t)"),
        )

        nc.sync.dma_start(y_rows[:, 3, :], y[:, 3, :])
        nc.sync.dma_start(out_1.rearrange("z l c r -> (z l) (c r)").bitcast(I32), y_codes[:].bitcast(I32))
        scale_rows = out_2.rearrange("z b c -> (z b) c").bitcast(I32)
        for quad in range(P // QUADRANT):
            queue = nc.scalar if quad < 3 else nc.sync
            queue.dma_start(
                scale_rows[SCALE_ROWS * quad : SCALE_ROWS * (quad + 1), :],
                y_scales[QUADRANT * quad : QUADRANT * quad + SCALE_ROWS, :].bitcast(I32),
            )
